import numpy as np
import ml_dtypes


def mxq(x, axis, fmt="e4m3"):
    dtype, down = {"e4m3": (ml_dtypes.float8_e4m3fn, 7), "e5m2": (ml_dtypes.float8_e5m2, 14)}[fmt]
    v = np.moveaxis(np.asarray(x, np.float32).astype(ml_dtypes.bfloat16).astype(np.float64), axis, -1)
    blocks = v.reshape(v.shape[:-1] + (-1, 32))
    amax = np.abs(blocks).max(-1, keepdims=True)
    byte = np.maximum(np.where(amax > 0, np.frexp(amax)[1] - 1 + 127, 0) - down, 1)
    scale = np.exp2(byte - 127.0)
    codes = (blocks / scale).astype(np.float32).astype(dtype).astype(np.float64)
    return np.moveaxis((codes * scale).reshape(v.shape), -1, axis)


WIDE = False


def mx_kscale(k):
    if not WIDE:
        return np.ones(k)
    levels = np.array([10, -10, 5, -5, 0])
    if k % 512:
        return np.exp2(np.random.permutation(np.resize(levels, k // 32))).repeat(32)
    a = np.empty((k // 512, 16))
    for p in range(k // 512):
        a[p, :8] = np.random.permutation(np.resize(levels, 8))
        for g in range(8):
            far = levels[np.abs(levels - a[p, g]) >= 10]
            a[p, g + 8] = far[np.random.randint(len(far))]
    return np.exp2(a.ravel()).repeat(32)


def f64(x):
    return np.asarray(x).astype(np.float64)


def striped(idx):
    return np.tile(idx.reshape(-1, 16).T, (8, 1)).astype(np.uint16)


def unstriped(offs):
    return offs[:16].T.reshape(-1).astype(np.int64)


E2M1 = np.array([0.0, 0.5, 1.0, 1.5, 2.0, 3.0, 4.0, 6.0, -0.0, -0.5, -1.0, -1.5, -2.0, -3.0, -4.0, -6.0])


def pack_weight(w, fmt):
    k, n = w.shape
    w = f64(np.asarray(w, np.float32).astype(ml_dtypes.bfloat16)).reshape(k // 32, 32, n)
    amax = np.abs(w).max(1)
    if fmt == "e4m3":
        byte = np.frexp(amax)[1] - 1 + 127 - 7
    else:
        mant, ex = np.frexp(amax / 6.0)
        byte = np.where(mant > 0.5, ex, ex - 1) + 127
    byte = np.clip(np.where(amax > 0, byte, 1), 1, 254)
    scaled = (w * np.exp2(127.0 - byte)[:, None, :]).reshape(k, n).astype(np.float32)
    by_word = np.ascontiguousarray(scaled.reshape(k // 512, 128, 4, n).transpose(0, 1, 3, 2))
    if fmt == "e4m3":
        words = by_word.astype(ml_dtypes.float8_e4m3fn).view(np.uint8)
    else:
        c = by_word.astype(ml_dtypes.float4_e2m1fn).view(np.uint8) & 0xF
        words = (c[..., 0::2] | (c[..., 1::2] << 4)).reshape(k // 512, 128, 2 * n)
    return np.ascontiguousarray(words), np.ascontiguousarray(byte.astype(np.uint8).reshape(k // 512, 16, n))


def unpack_weight(words, scales, fmt):
    g, _, n = scales.shape
    words = np.ascontiguousarray(words).reshape(g, 128, n, -1)
    if fmt == "e4m3":
        vals = words.view(ml_dtypes.float8_e4m3fn).astype(np.float64)
    else:
        nib = np.empty((g, 128, n, 4), np.uint8)
        nib[..., 0::2] = words & 0xF
        nib[..., 1::2] = words >> 4
        vals = E2M1[nib]
    vals = vals * np.repeat(np.exp2(scales.astype(np.float64) - 127.0), 8, axis=1)[..., None]
    return vals.transpose(0, 1, 3, 2).reshape(g * 512, n)


def gelu(v):
    return 0.5 * v * (1.0 + np.tanh(np.sqrt(2.0 / np.pi) * (v + 0.044715 * v**3)))


def often(T, S):
    return np.random.permutation(T)[(T * np.random.uniform(0, 1, S) ** 4).astype(np.int64)]


K, T, S, P, H, N = 512, 2048, 1024, 512, 1024, 384


def setup_inputs():
    n = np.random.standard_normal
    s = mx_kscale(K)[:, None]
    u = mx_kscale(H)[:, None]
    d = {}
    d["tab_words"], d["tab_scales"] = pack_weight(n((K, T)) * s, "e4m3")
    d["tab2_words"], d["tab2_scales"] = pack_weight(n((K, T)) * s, "e4m3")
    d["tab3_words"], d["tab3_scales"] = pack_weight(n((K, T)) * s, "e4m3")
    d["offs"] = striped(np.random.permutation(T)[:S])
    d["offs2"] = striped(np.random.permutation(T)[:S])
    d["offs3"] = striped(np.random.permutation(T)[:S])
    d["pos1"] = striped(np.random.permutation(S)[:P])
    d["pos2"] = striped(often(S, P))
    d["pos3"] = striped(often(S, P))
    d["wa"] = (n((K, H)) / s * u.T / K ** 0.5).astype(np.float32)
    d["wb_words"], d["wb_scales"] = pack_weight(n((K, H)) / s * u.T / K ** 0.5, "e2m1")
    d["wd"] = (n((K, H)) / s * u.T / K ** 0.5).astype(np.float32)
    d["wo_words"], d["wo_scales"] = pack_weight(0.8 * n((H, N)) / u / H ** 0.5, "e4m3")
    d["bo"] = (0.5 * n(N)).astype(np.float32)
    return d


def reference(tab_words, tab_scales, tab2_words, tab2_scales, tab3_words, tab3_scales,
              offs, offs2, offs3, pos1, pos2, pos3, wa, wb_words, wb_scales, wd,
              wo_words, wo_scales, bo):
    v = unpack_weight(tab_words, tab_scales, "e4m3")[:, unstriped(offs)]
    v2 = unpack_weight(tab2_words, tab2_scales, "e4m3")[:, unstriped(offs2)]
    v3 = unpack_weight(tab3_words, tab3_scales, "e4m3")[:, unstriped(offs3)]
    a = mxq(f64(wa), 0, "e4m3").T @ v
    b = unpack_weight(wb_words, wb_scales, "e2m1").T @ v2
    d = mxq(f64(wd), 0, "e4m3").T @ v3
    ap, bp, dp = a[:, unstriped(pos1)], b[:, unstriped(pos2)], d[:, unstriped(pos3)]
    z = np.maximum(np.maximum(ap + bp, ap + dp), bp + dp)
    y = unpack_weight(wo_words, wo_scales, "e4m3").T @ mxq(z, 0, "e4m3")
    return np.tanh(y + f64(bo)[:, None])

@@ -1,0 +1,283 @@
+from contextlib import ExitStack
+
+import concourse.mybir as mybir
+from concourse.masks import make_identity
+
+K, T, S, J, H, N = 512, 2048, 1024, 512, 1024, 384
+FLOPS = 2 * (3 * K * H * S + H * N * J)
+
+F32 = mybir.dt.float32
+BF16 = mybir.dt.bfloat16
+I32 = mybir.dt.int32
+U32 = mybir.dt.uint32
+U16 = mybir.dt.uint16
+U8 = mybir.dt.uint8
+FP8X4 = mybir.dt.float8_e4m3fn_x4
+FP4X4 = mybir.dt.float4_e2m1fn_x4
+ACT = mybir.ActivationFunctionType
+MAX = mybir.AluOpType.max
+
+P = 128
+PACK = 4
+BANK = 512
+ROW_TILES = H // P
+TILES_A_PASS = 4
+HALF = J // 2
+FIRST_SCALE_ROW = {"a": 4, "b": 0, "d": 8}
+
+
+def tile_list_trio_pair_max_kernel(
+    tc, tab_words, tab_scales, tab2_words, tab2_scales, tab3_words, tab3_scales,
+    offs, offs2, offs3, pos1, pos2, pos3, wa, wb_words, wb_scales, wd, wo_words, wo_scales, bo, out,
+):
+    nc = tc.nc
+    with ExitStack() as ctx:
+        keep = ctx.enter_context(tc.tile_pool(name="keep", bufs=1))
+        ring = ctx.enter_context(tc.tile_pool(name="ring", bufs=3))
+        psum = ctx.enter_context(tc.psum_pool(name="psum", bufs=2))
+
+        def load_list(dram, name):
+            tile = keep.tile(list(dram.shape), U16, name=name)
+            nc.sync.dma_start(tile[:], dram)
+            return tile
+
+        def load_scale_rows(queue, plane, rows, first=0):
+            for q in range(4):
+                lo = 32 * q + first
+                queue.dma_start(out=plane[lo : lo + 4].bitcast(I32), in_=rows[4 * q : 4 * q + 4].bitcast(I32))
+
+        def zeroed_plane(engine, shape, name):
+            plane = keep.tile(shape, U8, name=name, align_bytes=64)
+            engine.memset(plane[:].bitcast(I32), 0)
+            return plane
+
+        def load_table_words(dram, name):
+            words = keep.tile([P, T], U32, name=name, align_bytes=64)
+            nc.sync.dma_start(out=words[:].bitcast(I32), in_=dram[0].rearrange("p t i -> p (t i)").bitcast(I32))
+            return words
+
+        def load_weight_half(dram, half, name):
+            raw = keep.tile([P, PACK, BANK], F32, name=name)
+            nc.sync.dma_start(out=raw[:], in_=dram[:, half * BANK : (half + 1) * BANK].rearrange("(p i) c -> p i c", i=PACK))
+            return raw
+
+        scale_tab_b = zeroed_plane(nc.gpsimd, [P, T], "scale_tab_b")
+        wb_plane = zeroed_plane(nc.gpsimd, [P, H], "wb_plane")
+        scale_tab_a = zeroed_plane(nc.vector, [P, T], "scale_tab_a")
+        scale_tab_d = zeroed_plane(nc.vector, [P, T], "scale_tab_d")
+        wo_plane = zeroed_plane(nc.vector, [P, 2, N], "wo_plane")
+        raw = {}
+        list_b = load_list(offs2, "list_b")
+        load_scale_rows(nc.sync, scale_tab_b, tab2_scales[0], FIRST_SCALE_ROW["b"])
+        load_scale_rows(nc.gpsimd, wb_plane, wb_scales[0])
+        word_tab_b = load_table_words(tab2_words, "word_tab_b")
+        list_a = load_list(offs, "list_a")
+        wb_codes = keep.tile([P, 2 * H], U8, align_bytes=64)
+        nc.sync.dma_start(out=wb_codes[:].bitcast(I32), in_=wb_words[0].bitcast(I32))
+        load_scale_rows(nc.sync, scale_tab_a, tab_scales[0], FIRST_SCALE_ROW["a"])
+        word_tab_a = load_table_words(tab_words, "word_tab_a")
+        list_d = load_list(offs3, "list_d")
+        raw["a", 0] = load_weight_half(wa, 0, "raw_a0")
+        load_scale_rows(nc.sync, scale_tab_d, tab3_scales[0], FIRST_SCALE_ROW["d"])
+        word_tab_d = load_table_words(tab3_words, "word_tab_d")
+        pick_b = load_list(pos2, "pick_b")
+        raw["d", 0] = load_weight_half(wd, 0, "raw_d0")
+        raw["a", 1] = load_weight_half(wa, 1, "raw_a1")
+        raw["d", 1] = load_weight_half(wd, 1, "raw_d1")
+        pick_a = load_list(pos1, "pick_a")
+        pick_d = load_list(pos3, "pick_d")
+        wo_codes = keep.tile([P, 2, N], U32, align_bytes=64)
+        nc.sync.dma_start(out=wo_codes[:].bitcast(I32), in_=wo_words.rearrange("g p c i -> p g (c i)").bitcast(I32))
+        load_scale_rows(nc.sync, wo_plane, wo_scales.rearrange("g q c -> q g c"))
+        bias = keep.tile([P, N // P], F32)
+        with nc.allow_non_contiguous_dma(reason="one bias value for each partition"):
+            nc.sync.dma_start(out=bias[:], in_=bo.rearrange("(c p) -> p c", p=P))
+        identity = keep.tile([P, P], F32)
+        make_identity(nc, identity[:])
+
+        def gather_scales(plane, entries, name):
+            picked = keep.tile([P, S], U8, name=name, align_bytes=64)
+            nc.vector.tensor_copy(picked[:], plane[:].indirect(entries[:]))
+            return picked
+
+        def gather_words(words, entries, name):
+            halves = []
+            for half in range(2):
+                picked = keep.tile([P, BANK], U32, name=f"{name}{half}", align_bytes=64)
+                nc.vector.tensor_copy(picked[:], words[:].indirect(entries[:, half * 32 : (half + 1) * 32]))
+                halves.append(picked)
+            return halves
+
+        moving_scales, moving_words = {}, {}
+        for name, plane, words, entries in (
+            ("b", scale_tab_b, word_tab_b, list_b), ("a", scale_tab_a, word_tab_a, list_a), ("d", scale_tab_d, word_tab_d, list_d),
+        ):
+            moving_scales[name] = gather_scales(plane, entries, f"scales_{name}")
+            moving_words[name] = gather_words(words, entries, f"words_{name}")
+
+        rounded, codes, planes = {}, {}, {}
+
+        def round_weight(name, half):
+            rounded[name, half] = keep.tile([P, BANK, PACK], BF16, name=f"rounded_{name}{half}", align_bytes=64)
+            nc.scalar.activation(
+                out=rounded[name, half][:].rearrange("p (c e) i -> p c i e", e=4),
+                in_=raw[name, half][:].rearrange("p i (c e) -> p c i e", e=4),
+                func=ACT.Copy,
+            )
+
+        def quantise(values, name):
+            width = values.shape[1]
+            words = keep.tile([P, width], U32, name=f"codes_{name}", align_bytes=64)
+            plane = keep.tile([P, width], U8, name=f"plane_{name}", align_bytes=64)
+            nc.vector.quantize_mx(out=words[:].bitcast(FP8X4), scales=plane[:], in_=values[:].rearrange("p c i -> p (c i)"))
+            return words, plane
+
+        def quantise_weight(name, half):
+            codes[name, half], planes[name, half] = quantise(rounded[name, half], f"{name}{half}")
+
+        features = {}
+
+        def first_stage(name, t):
+            if name == "b":
+                lhs = wb_codes[:, 2 * P * t : 2 * P * (t + 1)].bitcast(FP4X4)
+                lhs_plane = wb_plane[:, P * t : P * (t + 1)]
+            else:
+                half, cols = t // TILES_A_PASS, slice(P * (t % TILES_A_PASS), P * (t % TILES_A_PASS + 1))
+                lhs = codes[name, half][:, cols].bitcast(FP8X4)
+                lhs_plane = planes[name, half][:, cols]
+            rows = ring.tile([P, S], F32, name=f"rows_{name}", bufs=6 if name == "b" else 3)
+            for half in range(2):
+                cols = slice(half * BANK, (half + 1) * BANK)
+                acc = psum.tile([P, BANK], F32, name="acc", bufs=4)
+                nc.tensor.matmul_mx(
+                    out=acc[:], lhsT=lhs, lhsT_scale=lhs_plane,
+                    rhs=moving_words[name][half][:].bitcast(FP8X4), rhs_scale=moving_scales[name][FIRST_SCALE_ROW[name] :, cols],
+                    start=True, stop=True,
+                )
+                nc.scalar.copy(out=rows[:, cols], in_=acc[:])
+            features[name, t] = rows
+
+        picked = {}
+        picks = {"a": pick_a, "b": pick_b, "d": pick_d}
+
+        def pick(name, t, pieces=1):
+            picked[name, t] = ring.tile([P, J], F32, name=f"picked_{name}", bufs=ROW_TILES if name == "b" else 3)
+            step = J // pieces
+            for lo in range(0, J, step):
+                nc.vector.tensor_copy(
+                    picked[name, t][:, lo : lo + step],
+                    features[name, t][:].indirect(picks[name][:, lo // 16 : (lo + step) // 16]),
+                )
+
+        def larger_of_b_d(t):
+            picked["m", t] = ring.tile([P, J], F32, name="larger")
+            nc.vector.tensor_tensor(picked["m", t][:], picked["b", t][:], picked["d", t][:], MAX)
+
+        def turned_sum(first, second, t, tag):
+            total = psum.tile([P, J // P, P], F32, name=tag)
+            for block in range(J // P):
+                cols = slice(block * P, (block + 1) * P)
+                nc.tensor.matmul(total[:, block, :], picked[first, t][:, cols], identity[:], is_transpose=True, start=True, stop=False)
+                nc.tensor.matmul(total[:, block, :], picked[second, t][:, cols], identity[:], is_transpose=True, start=False, stop=True)
+            return total
+
+        sums = {}
+
+        def sum_b_d(t):
+            total = turned_sum("b", "d", t, "spare")
+            sums["s", t] = ring.tile([P, J // P, P], F32, name="sum_bd")
+            nc.scalar.copy(out=sums["s", t][:], in_=total[:])
+
+        def sum_with_a(t):
+            sums["t", t] = turned_sum("m", "a", t, "with_a")
+
+        z_turned = {
+            (g, half): keep.tile([P, 2, BANK], BF16, name=f"z_turned{g}{half}") for g in range(2) for half in range(2)
+        }
+
+        def finish_z(t):
+            g, cols = t // TILES_A_PASS, slice(P * (t % TILES_A_PASS), P * (t % TILES_A_PASS + 1))
+            for half in range(2):
+                blocks = slice(2 * half, 2 * half + 2)
+                nc.vector.tensor_tensor(z_turned[g, half][:, :, cols], sums["t", t][:, blocks, :], sums["s", t][:, blocks, :], MAX)
+
+        z_rounded, z_codes, z_planes = {}, {}, {}
+
+        def turn_back(g, half):
+            pairs = z_turned[g, half][:].bitcast(F32)
+            back = psum.tile([P, 2, 2, P], F32, name="spare")
+            for block in range(2):
+                for u in range(2):
+                    nc.tensor.transpose(back[:, block, u, :], pairs[:, block, u::2], identity[:])
+            z_rounded[g, half] = keep.tile([P, HALF, PACK], BF16, name=f"z_rounded{g}{half}", align_bytes=64)
+            nc.scalar.copy(
+                out=z_rounded[g, half][:].bitcast(F32).rearrange("p (b j) u -> p b j u", b=2),
+                in_=back[:].rearrange("p b u j -> p b j u"),
+            )
+
+        def quantise_z(g, half):
+            z_codes[g, half], z_planes[g, half] = quantise(z_rounded[g, half], f"z{g}{half}")
+
+        def second_stage_pass(banks, g, half):
+            for c in range(N // P):
+                cols = slice(c * P, (c + 1) * P)
+                nc.tensor.matmul_mx(
+                    out=banks[c // 2][:, c % 2, :], lhsT=wo_codes[:, g, cols].bitcast(FP8X4), lhsT_scale=wo_plane[:, g, cols],
+                    rhs=z_codes[g, half][:].bitcast(FP8X4), rhs_scale=z_planes[g, half][:],
+                    start=(g == 0 and c % 2 == 0), stop=(g == 1 and c != 0),
+                )
+
+        def finish(banks, half):
+            for c in range(N // P):
+                result = keep.tile([P, HALF], F32, name=f"result{half}{c}")
+                nc.scalar.activation(out=result[:], in_=banks[c // 2][:, c % 2, :], func=ACT.Tanh, bias=bias[:, c : c + 1])
+                nc.sync.dma_start(out=out[c * P : (c + 1) * P, half * HALF : (half + 1) * HALF], in_=result[:])
+
+        for t in range(ROW_TILES):
+            first_stage("b", t)
+            if t == 1:
+                round_weight("a", 0)
+            if t == 5:
+                round_weight("d", 0)
+                quantise_weight("a", 0)
+            pick("b", t)
+        quantise_weight("d", 0)
+        first_stage("a", 0)
+        first_stage("d", 0)
+        last = ROW_TILES - 1
+        for t in range(ROW_TILES):
+            if t == last:
+                pick("d", t)
+                finish_z(t - 1)
+                larger_of_b_d(t)
+                pick("a", t, pieces=2)
+            else:
+                pick("a", t)
+                pick("d", t)
+                if t > 0:
+                    finish_z(t - 1)
+                larger_of_b_d(t)
+                first_stage("a", t + 1)
+                first_stage("d", t + 1)
+            if t < 2:
+                round_weight("ad"[t], 1)
+            if 1 <= t < 3:
+                quantise_weight("ad"[t - 1], 1)
+            if t == TILES_A_PASS:
+                turn_back(0, 0)
+                turn_back(0, 1)
+            if t == TILES_A_PASS + 1:
+                quantise_z(0, 0)
+                quantise_z(0, 1)
+            sum_b_d(t)
+            sum_with_a(t)
+        banks = [[psum.tile([P, 2, HALF], F32, name="acc", bufs=4) for c in range(2)] for half in range(2)]
+        for half in range(2):
+            second_stage_pass(banks[half], 0, half)
+        finish_z(last)
+        for half in range(2):
+            turn_back(1, half)
+        for half in range(2):
+            quantise_z(1, half)
+            second_stage_pass(banks[half], 1, half)
+            finish(banks[half], half)

@@ -22,7 +22,8 @@ PACK = 4
 BANK = 512
 ROW_TILES = H // P
 TILES_A_PASS = 4
-HALF = J // 2
+BLOCKS = J // P
+TAIL = (slice(0, 2), slice(2, 3), slice(3, 4))
 FIRST_SCALE_ROW = {"a": 4, "b": 0, "d": 8}
 
 
@@ -34,7 +35,10 @@ def tile_list_trio_pair_max_kernel(
     with ExitStack() as ctx:
         keep = ctx.enter_context(tc.tile_pool(name="keep", bufs=1))
         ring = ctx.enter_context(tc.tile_pool(name="ring", bufs=3))
+        reused = ctx.enter_context(tc.tile_pool(name="reused", bufs=1))
         psum = ctx.enter_context(tc.psum_pool(name="psum", bufs=2))
+
+        raw = {}
 
         def load_list(dram, name):
             tile = keep.tile(list(dram.shape), U16, name=name)
@@ -56,36 +60,38 @@ def tile_list_trio_pair_max_kernel(
             nc.sync.dma_start(out=words[:].bitcast(I32), in_=dram[0].rearrange("p t i -> p (t i)").bitcast(I32))
             return words
 
-        def load_weight_half(dram, half, name):
-            raw = keep.tile([P, PACK, BANK], F32, name=name)
-            nc.sync.dma_start(out=raw[:], in_=dram[:, half * BANK : (half + 1) * BANK].rearrange("(p i) c -> p i c", i=PACK))
-            return raw
+        def load_weight(dram, name, lo, hi):
+            if (name, lo) == ("a", 0):
+                raw[name, lo, hi] = reused.tile([P, PACK, hi - lo], F32, name="raw_a0", offset=0)
+            else:
+                raw[name, lo, hi] = keep.tile([P, PACK, hi - lo], F32, name=f"raw_{name}{lo}")
+            nc.sync.dma_start(out=raw[name, lo, hi][:], in_=dram[:, lo:hi].rearrange("(p i) c -> p i c", i=PACK))
 
         scale_tab_b = zeroed_plane(nc.gpsimd, [P, T], "scale_tab_b")
         wb_plane = zeroed_plane(nc.gpsimd, [P, H], "wb_plane")
-        scale_tab_a = zeroed_plane(nc.vector, [P, T], "scale_tab_a")
         scale_tab_d = zeroed_plane(nc.vector, [P, T], "scale_tab_d")
+        scale_tab_a = zeroed_plane(nc.vector, [P, T], "scale_tab_a")
         wo_plane = zeroed_plane(nc.vector, [P, 2, N], "wo_plane")
-        raw = {}
         list_b = load_list(offs2, "list_b")
-        load_scale_rows(nc.sync, scale_tab_b, tab2_scales[0], FIRST_SCALE_ROW["b"])
-        load_scale_rows(nc.gpsimd, wb_plane, wb_scales[0])
-        word_tab_b = load_table_words(tab2_words, "word_tab_b")
         list_a = load_list(offs, "list_a")
+        list_d = load_list(offs3, "list_d")
+        pick_b = load_list(pos2, "pick_b")
+        word_tab_b = load_table_words(tab2_words, "word_tab_b")
         wb_codes = keep.tile([P, 2 * H], U8, align_bytes=64)
         nc.sync.dma_start(out=wb_codes[:].bitcast(I32), in_=wb_words[0].bitcast(I32))
-        load_scale_rows(nc.sync, scale_tab_a, tab_scales[0], FIRST_SCALE_ROW["a"])
-        word_tab_a = load_table_words(tab_words, "word_tab_a")
-        list_d = load_list(offs3, "list_d")
-        raw["a", 0] = load_weight_half(wa, 0, "raw_a0")
-        load_scale_rows(nc.sync, scale_tab_d, tab3_scales[0], FIRST_SCALE_ROW["d"])
-        word_tab_d = load_table_words(tab3_words, "word_tab_d")
-        pick_b = load_list(pos2, "pick_b")
-        raw["d", 0] = load_weight_half(wd, 0, "raw_d0")
-        raw["a", 1] = load_weight_half(wa, 1, "raw_a1")
-        raw["d", 1] = load_weight_half(wd, 1, "raw_d1")
-        pick_a = load_list(pos1, "pick_a")
+        load_weight(wd, "d", 0, BANK // 2)
         pick_d = load_list(pos3, "pick_d")
+        load_scale_rows(nc.sync, scale_tab_b, tab2_scales[0], FIRST_SCALE_ROW["b"])
+        word_tab_d = load_table_words(tab3_words, "word_tab_d")
+        load_scale_rows(nc.sync, wb_plane, wb_scales[0])
+        load_weight(wd, "d", BANK // 2, BANK)
+        word_tab_a = load_table_words(tab_words, "word_tab_a")
+        load_scale_rows(nc.sync, scale_tab_d, tab3_scales[0], FIRST_SCALE_ROW["d"])
+        load_weight(wa, "a", 0, BANK)
+        load_scale_rows(nc.sync, scale_tab_a, tab_scales[0], FIRST_SCALE_ROW["a"])
+        load_weight(wd, "d", BANK, H)
+        load_weight(wa, "a", BANK, H)
+        pick_a = load_list(pos1, "pick_a")
         wo_codes = keep.tile([P, 2, N], U32, align_bytes=64)
         nc.sync.dma_start(out=wo_codes[:].bitcast(I32), in_=wo_words.rearrange("g p c i -> p g (c i)").bitcast(I32))
         load_scale_rows(nc.sync, wo_plane, wo_scales.rearrange("g q c -> q g c"))
@@ -95,33 +101,33 @@ def tile_list_trio_pair_max_kernel(
         identity = keep.tile([P, P], F32)
         make_identity(nc, identity[:])
 
-        def gather_scales(plane, entries, name):
-            picked = keep.tile([P, S], U8, name=name, align_bytes=64)
-            nc.vector.tensor_copy(picked[:], plane[:].indirect(entries[:]))
-            return picked
+        moving_words, moving_scales = {}, {}
 
-        def gather_words(words, entries, name):
-            halves = []
-            for half in range(2):
-                picked = keep.tile([P, BANK], U32, name=f"{name}{half}", align_bytes=64)
-                nc.vector.tensor_copy(picked[:], words[:].indirect(entries[:, half * 32 : (half + 1) * 32]))
-                halves.append(picked)
-            return halves
+        def gather_table(name, words, plane, entries, pieces):
+            step = S // pieces
+            for lo in range(0, S, step):
+                part = entries[:, lo // 16 : (lo + step) // 16]
+                picked_words = keep.tile([P, step], U32, name=f"words_{name}{lo}", align_bytes=64)
+                nc.vector.tensor_copy(picked_words[:], words[:].indirect(part))
+                picked_scales = keep.tile([P, step], U8, name=f"scales_{name}{lo}", align_bytes=64)
+                nc.vector.tensor_copy(picked_scales[:], plane[:].indirect(part))
+                for at in range(0, step, BANK):
+                    moving_words[name, (lo + at) // BANK] = picked_words[:, at : at + BANK].bitcast(FP8X4)
+                    moving_scales[name, (lo + at) // BANK] = picked_scales[FIRST_SCALE_ROW[name] :, at : at + BANK]
 
-        moving_scales, moving_words = {}, {}
-        for name, plane, words, entries in (
-            ("b", scale_tab_b, word_tab_b, list_b), ("a", scale_tab_a, word_tab_a, list_a), ("d", scale_tab_d, word_tab_d, list_d),
-        ):
-            moving_scales[name] = gather_scales(plane, entries, f"scales_{name}")
-            moving_words[name] = gather_words(words, entries, f"words_{name}")
+        gather_table("b", word_tab_b, scale_tab_b, list_b, 2)
+        gather_table("d", word_tab_d, scale_tab_d, list_d, 1)
+        gather_table("a", word_tab_a, scale_tab_a, list_a, 1)
 
         rounded, codes, planes = {}, {}, {}
 
-        def round_weight(name, half):
-            rounded[name, half] = keep.tile([P, BANK, PACK], BF16, name=f"rounded_{name}{half}", align_bytes=64)
+        def round_weight(name, lo, hi):
+            g, at = divmod(lo, BANK)
+            if at == 0:
+                rounded[name, g] = keep.tile([P, BANK, PACK], BF16, name=f"rounded_{name}{g}", align_bytes=64)
             nc.scalar.activation(
-                out=rounded[name, half][:].rearrange("p (c e) i -> p c i e", e=4),
-                in_=raw[name, half][:].rearrange("p i (c e) -> p c i e", e=4),
+                out=rounded[name, g][:, at : at + hi - lo, :].rearrange("p (c e) i -> p c i e", e=4),
+                in_=raw[name, lo, hi][:].rearrange("p i (c e) -> p c i e", e=4),
                 func=ACT.Copy,
             )
 
@@ -137,147 +143,163 @@ def tile_list_trio_pair_max_kernel(
 
         features = {}
 
-        def first_stage(name, t):
+        def first_stage_half(name, t, half):
             if name == "b":
                 lhs = wb_codes[:, 2 * P * t : 2 * P * (t + 1)].bitcast(FP4X4)
                 lhs_plane = wb_plane[:, P * t : P * (t + 1)]
             else:
-                half, cols = t // TILES_A_PASS, slice(P * (t % TILES_A_PASS), P * (t % TILES_A_PASS + 1))
-                lhs = codes[name, half][:, cols].bitcast(FP8X4)
-                lhs_plane = planes[name, half][:, cols]
-            rows = ring.tile([P, S], F32, name=f"rows_{name}", bufs=6 if name == "b" else 3)
+                g, cols = t // TILES_A_PASS, slice(P * (t % TILES_A_PASS), P * (t % TILES_A_PASS + 1))
+                lhs = codes[name, g][:, cols].bitcast(FP8X4)
+                lhs_plane = planes[name, g][:, cols]
+            if half == 0 and name == "b" and t >= 6:
+                features[name, t] = reused.tile([P, S], F32, name=f"rows_b{t}", offset=(t - 6) * S * 4)
+            elif half == 0:
+                features[name, t] = ring.tile([P, S], F32, name=f"rows_{name}", bufs=6 if name == "b" else 3)
+            acc = psum.tile([P, BANK], F32, name="acc", bufs=4)
+            nc.tensor.matmul_mx(
+                out=acc[:], lhsT=lhs, lhsT_scale=lhs_plane,
+                rhs=moving_words[name, half], rhs_scale=moving_scales[name, half], start=True, stop=True,
+            )
+            nc.scalar.copy(out=features[name, t][:, half * BANK : (half + 1) * BANK], in_=acc[:])
+
+        def first_stage(name, t):
             for half in range(2):
-                cols = slice(half * BANK, (half + 1) * BANK)
-                acc = psum.tile([P, BANK], F32, name="acc", bufs=4)
-                nc.tensor.matmul_mx(
-                    out=acc[:], lhsT=lhs, lhsT_scale=lhs_plane,
-                    rhs=moving_words[name][half][:].bitcast(FP8X4), rhs_scale=moving_scales[name][FIRST_SCALE_ROW[name] :, cols],
-                    start=True, stop=True,
-                )
-                nc.scalar.copy(out=rows[:, cols], in_=acc[:])
-            features[name, t] = rows
+                first_stage_half(name, t, half)
 
         picked = {}
         picks = {"a": pick_a, "b": pick_b, "d": pick_d}
 
-        def pick(name, t, pieces=1):
-            picked[name, t] = ring.tile([P, J], F32, name=f"picked_{name}", bufs=ROW_TILES if name == "b" else 3)
-            step = J // pieces
-            for lo in range(0, J, step):
-                nc.vector.tensor_copy(
-                    picked[name, t][:, lo : lo + step],
-                    features[name, t][:].indirect(picks[name][:, lo // 16 : (lo + step) // 16]),
-                )
+        def pick(name, t, blocks=slice(0, BLOCKS)):
+            if blocks.start == 0:
+                picked[name, t] = ring.tile([P, J], F32, name=f"picked_{name}", bufs=ROW_TILES if name == "b" else 3)
+            lo, hi = blocks.start * P, blocks.stop * P
+            nc.vector.tensor_copy(picked[name, t][:, lo:hi], features[name, t][:].indirect(picks[name][:, lo // 16 : hi // 16]))
 
-        def larger_of_b_d(t):
-            picked["m", t] = ring.tile([P, J], F32, name="larger")
-            nc.vector.tensor_tensor(picked["m", t][:], picked["b", t][:], picked["d", t][:], MAX)
+        def larger_of_b_d(t, blocks=slice(0, BLOCKS)):
+            if blocks.start == 0:
+                picked["m", t] = ring.tile([P, J], F32, name="larger")
+            cols = slice(blocks.start * P, blocks.stop * P)
+            nc.vector.tensor_tensor(picked["m", t][:, cols], picked["b", t][:, cols], picked["d", t][:, cols], MAX)
 
-        def turned_sum(first, second, t, tag):
-            total = psum.tile([P, J // P, P], F32, name=tag)
-            for block in range(J // P):
+        def turned_sum(first, second, t, blocks, tag):
+            total = psum.tile([P, blocks.stop - blocks.start, P], F32, name=tag)
+            for at, block in enumerate(range(blocks.start, blocks.stop)):
                 cols = slice(block * P, (block + 1) * P)
-                nc.tensor.matmul(total[:, block, :], picked[first, t][:, cols], identity[:], is_transpose=True, start=True, stop=False)
-                nc.tensor.matmul(total[:, block, :], picked[second, t][:, cols], identity[:], is_transpose=True, start=False, stop=True)
+                nc.tensor.matmul(total[:, at, :], picked[first, t][:, cols], identity[:], is_transpose=True, start=True, stop=False)
+                nc.tensor.matmul(total[:, at, :], picked[second, t][:, cols], identity[:], is_transpose=True, start=False, stop=True)
             return total
 
         sums = {}
 
         def sum_b_d(t):
-            total = turned_sum("b", "d", t, "spare")
-            sums["s", t] = ring.tile([P, J // P, P], F32, name="sum_bd")
+            total = turned_sum("b", "d", t, slice(0, BLOCKS), "spare")
+            sums["s", t] = ring.tile([P, BLOCKS, P], F32, name="sum_bd")
             nc.scalar.copy(out=sums["s", t][:], in_=total[:])
 
-        def sum_with_a(t):
-            sums["t", t] = turned_sum("m", "a", t, "with_a")
+        def sum_with_a(t, blocks):
+            sums["t", t, blocks.start] = turned_sum("m", "a", t, blocks, "with_a")
 
-        z_turned = {
-            (g, half): keep.tile([P, 2, BANK], BF16, name=f"z_turned{g}{half}") for g in range(2) for half in range(2)
-        }
+        z_turned = [keep.tile([P, BLOCKS * BANK], BF16, name=f"z_turned{g}") for g in range(2)]
 
-        def finish_z(t):
+        def finish_z(t, blocks=slice(0, BLOCKS)):
             g, cols = t // TILES_A_PASS, slice(P * (t % TILES_A_PASS), P * (t % TILES_A_PASS + 1))
-            for half in range(2):
-                blocks = slice(2 * half, 2 * half + 2)
-                nc.vector.tensor_tensor(z_turned[g, half][:, :, cols], sums["t", t][:, blocks, :], sums["s", t][:, blocks, :], MAX)
+            target = z_turned[g][:].rearrange("p (b r) -> p b r", b=BLOCKS)[:, blocks, cols]
+            nc.vector.tensor_tensor(target, sums["t", t, blocks.start][:], sums["s", t][:, blocks, :], MAX)
 
-        z_rounded, z_codes, z_planes = {}, {}, {}
-
-        def turn_back(g, half):
-            pairs = z_turned[g, half][:].bitcast(F32)
-            back = psum.tile([P, 2, 2, P], F32, name="spare")
-            for block in range(2):
+        def turn_back(g, blocks, target, copy):
+            pairs = z_turned[g][:].bitcast(F32)
+            count = blocks.stop - blocks.start
+            back = psum.tile([P, count, 2, P], F32, name="spare")
+            for at in range(count):
+                lo = (blocks.start + at) * BANK // 2
                 for u in range(2):
-                    nc.tensor.transpose(back[:, block, u, :], pairs[:, block, u::2], identity[:])
-            z_rounded[g, half] = keep.tile([P, HALF, PACK], BF16, name=f"z_rounded{g}{half}", align_bytes=64)
-            nc.scalar.copy(
-                out=z_rounded[g, half][:].bitcast(F32).rearrange("p (b j) u -> p b j u", b=2),
+                    nc.tensor.transpose(back[:, at, u, :], pairs[:, lo + u : lo + BANK // 2 : 2], identity[:])
+            copy(
+                out=target.bitcast(F32).rearrange("p (b j) u -> p b j u", b=count),
                 in_=back[:].rearrange("p b u j -> p b j u"),
             )
 
-        def quantise_z(g, half):
-            z_codes[g, half], z_planes[g, half] = quantise(z_rounded[g, half], f"z{g}{half}")
+        def open_banks(width):
+            per_bank = min(BANK // width, N // P)
+            slots = []
+            for lo in range(0, N // P, per_bank):
+                bank = psum.tile([P, BANK], F32, name="acc", bufs=4)
+                count = min(per_bank, N // P - lo)
+                slots.extend((bank[:, at * width : (at + 1) * width], at == 0, at == count - 1) for at in range(count))
+            return slots
 
-        def second_stage_pass(banks, g, half):
-            for c in range(N // P):
+        def second_stage_pass(slots, g, z_words, z_plane):
+            for c, (acc, first, final) in enumerate(slots):
                 cols = slice(c * P, (c + 1) * P)
                 nc.tensor.matmul_mx(
-                    out=banks[c // 2][:, c % 2, :], lhsT=wo_codes[:, g, cols].bitcast(FP8X4), lhsT_scale=wo_plane[:, g, cols],
-                    rhs=z_codes[g, half][:].bitcast(FP8X4), rhs_scale=z_planes[g, half][:],
-                    start=(g == 0 and c % 2 == 0), stop=(g == 1 and c != 0),
+                    out=acc, lhsT=wo_codes[:, g, cols].bitcast(FP8X4), lhsT_scale=wo_plane[:, g, cols],
+                    rhs=z_words.bitcast(FP8X4), rhs_scale=z_plane,
+                    start=(g == 0 and first), stop=(g == 1 and final),
                 )
 
-        def finish(banks, half):
-            for c in range(N // P):
-                result = keep.tile([P, HALF], F32, name=f"result{half}{c}")
-                nc.scalar.activation(out=result[:], in_=banks[c // 2][:, c % 2, :], func=ACT.Tanh, bias=bias[:, c : c + 1])
-                nc.sync.dma_start(out=out[c * P : (c + 1) * P, half * HALF : (half + 1) * HALF], in_=result[:])
+        def finish(slots, blocks):
+            cols = slice(blocks.start * P, blocks.stop * P)
+            result = keep.tile([P, N // P, cols.stop - cols.start], F32, name=f"result{blocks.start}")
+            for c, (acc, first, final) in enumerate(slots):
+                nc.scalar.activation(out=result[:, c, :], in_=acc, func=ACT.Tanh, bias=bias[:, c : c + 1])
+            nc.sync.dma_start(out=out[:, cols].rearrange("(c p) j -> p c j", p=P), in_=result[:])
 
+        round_weight("d", 0, BANK // 2)
+        for t in range(4):
+            first_stage_half("b", t, 0)
         for t in range(ROW_TILES):
-            first_stage("b", t)
+            if t >= 4:
+                first_stage_half("b", t, 0)
+            first_stage_half("b", t, 1)
             if t == 1:
-                round_weight("a", 0)
+                round_weight("d", BANK // 2, BANK)
             if t == 5:
-                round_weight("d", 0)
+                round_weight("a", 0, BANK)
+                quantise_weight("d", 0)
                 quantise_weight("a", 0)
             pick("b", t)
-        quantise_weight("d", 0)
-        first_stage("a", 0)
+        for name in "da":
+            round_weight(name, BANK, H)
+            quantise_weight(name, 1)
         first_stage("d", 0)
+        first_stage("a", 0)
         last = ROW_TILES - 1
-        for t in range(ROW_TILES):
-            if t == last:
-                pick("d", t)
+        z_rounded = keep.tile([P, J, PACK], BF16, align_bytes=64)
+        for t in range(last):
+            pick("d", t)
+            larger_of_b_d(t)
+            pick("a", t)
+            if t > 0:
                 finish_z(t - 1)
-                larger_of_b_d(t)
-                pick("a", t, pieces=2)
-            else:
-                pick("a", t)
-                pick("d", t)
-                if t > 0:
-                    finish_z(t - 1)
-                larger_of_b_d(t)
-                first_stage("a", t + 1)
-                first_stage("d", t + 1)
-            if t < 2:
-                round_weight("ad"[t], 1)
-            if 1 <= t < 3:
-                quantise_weight("ad"[t - 1], 1)
-            if t == TILES_A_PASS:
-                turn_back(0, 0)
-                turn_back(0, 1)
-            if t == TILES_A_PASS + 1:
-                quantise_z(0, 0)
-                quantise_z(0, 1)
+            first_stage("d", t + 1)
+            first_stage("a", t + 1)
             sum_b_d(t)
-            sum_with_a(t)
-        banks = [[psum.tile([P, 2, HALF], F32, name="acc", bufs=4) for c in range(2)] for half in range(2)]
-        for half in range(2):
-            second_stage_pass(banks[half], 0, half)
-        finish_z(last)
-        for half in range(2):
-            turn_back(1, half)
-        for half in range(2):
-            quantise_z(1, half)
-            second_stage_pass(banks[half], 1, half)
-            finish(banks[half], half)
+            sum_with_a(t, slice(0, BLOCKS))
+            if t == TILES_A_PASS:
+                for lo in range(0, BLOCKS, 2):
+                    turn_back(0, slice(lo, lo + 2), z_rounded[:, lo * P : (lo + 2) * P, :], nc.scalar.copy)
+            if t == TILES_A_PASS + 1:
+                z_words, z_plane = quantise(z_rounded, "z")
+        pick("d", last)
+        larger_of_b_d(last)
+        sum_b_d(last)
+        slots = {}
+        for blocks in TAIL:
+            cols = slice(blocks.start * P, blocks.stop * P)
+            slots[blocks.start] = open_banks(cols.stop - cols.start)
+            second_stage_pass(slots[blocks.start], 0, z_words[:, cols], z_plane[:, cols])
+        for blocks in TAIL:
+            pick("a", last, blocks)
+            if blocks.start == 0:
+                finish_z(last - 1)
+            sum_with_a(last, blocks)
+        tail_rounded = {}
+        for blocks in TAIL:
+            finish_z(last, blocks)
+            width = (blocks.stop - blocks.start) * P
+            tail_rounded[blocks.start] = keep.tile([P, width, PACK], BF16, name=f"tail_rounded{blocks.start}", align_bytes=64)
+            turn_back(1, blocks, tail_rounded[blocks.start][:], nc.scalar.copy if blocks.start == 0 else nc.vector.tensor_copy)
+        for blocks in TAIL:
+            tail_words, tail_plane = quantise(tail_rounded[blocks.start], f"tail{blocks.start}")
+            second_stage_pass(slots[blocks.start], 1, tail_words[:], tail_plane[:])
+            finish(slots[blocks.start], blocks)

@@ -19,12 +19,23 @@ MAX = mybir.AluOpType.max
 
 P = 128
 PACK = 4
+PASS = P * PACK
 BANK = 512
+GROUP = 16
+PASSES = H // PASS
 ROW_TILES = H // P
-TILES_A_PASS = 4
+TILES_A_PASS = PASS // P
 BLOCKS = J // P
-TAIL = (slice(0, 2), slice(2, 3), slice(3, 4))
+ALL_BLOCKS = slice(0, BLOCKS)
+BLOCK_PAIRS = (slice(0, 2), slice(2, 4))
+OUT_TILES = N // P
+
 FIRST_SCALE_ROW = {"a": 4, "b": 0, "d": 8}
+
+ACC_BANKS = 4
+OWN_B_TILES = 6
+ROUND_D_AFTER = 1
+LATE_PIECES = 2
 
 
 def tile_list_trio_pair_max_kernel(
@@ -45,57 +56,60 @@ def tile_list_trio_pair_max_kernel(
             nc.sync.dma_start(tile[:], dram)
             return tile
 
-        def load_scale_rows(queue, plane, rows, first=0):
-            for q in range(4):
-                lo = 32 * q + first
-                queue.dma_start(out=plane[lo : lo + 4].bitcast(I32), in_=rows[4 * q : 4 * q + 4].bitcast(I32))
-
         def zeroed_plane(engine, shape, name):
             plane = keep.tile(shape, U8, name=name, align_bytes=64)
             engine.memset(plane[:].bitcast(I32), 0)
             return plane
+
+        def load_scale_rows(plane, rows, first=0):
+            for quadrant in range(4):
+                lo = 32 * quadrant + first
+                nc.sync.dma_start(
+                    out=plane[lo : lo + 4].bitcast(I32), in_=rows[4 * quadrant : 4 * quadrant + 4].bitcast(I32)
+                )
 
         def load_table_words(dram, name):
             words = keep.tile([P, T], U32, name=name, align_bytes=64)
             nc.sync.dma_start(out=words[:].bitcast(I32), in_=dram[0].rearrange("p t i -> p (t i)").bitcast(I32))
             return words
 
-        def load_weight(dram, name, lo, hi):
-            if (name, lo) == ("a", 0):
-                raw[name, lo, hi] = reused.tile([P, PACK, hi - lo], F32, name="raw_a0", offset=0)
+        def load_weight(dram, name, g):
+            if (name, g) == ("a", 0):
+                raw[name, g] = reused.tile([P, PACK, PASS], F32, name="raw_a0", offset=0)
             else:
-                raw[name, lo, hi] = keep.tile([P, PACK, hi - lo], F32, name=f"raw_{name}{lo}")
-            nc.sync.dma_start(out=raw[name, lo, hi][:], in_=dram[:, lo:hi].rearrange("(p i) c -> p i c", i=PACK))
+                raw[name, g] = keep.tile([P, PACK, PASS], F32, name=f"raw_{name}{g}")
+            columns = dram[:, g * PASS : (g + 1) * PASS]
+            nc.sync.dma_start(out=raw[name, g][:], in_=columns.rearrange("(p i) c -> p i c", i=PACK))
 
-        scale_tab_b = zeroed_plane(nc.gpsimd, [P, T], "scale_tab_b")
+        table_scales_b = zeroed_plane(nc.gpsimd, [P, T], "table_scales_b")
         wb_plane = zeroed_plane(nc.gpsimd, [P, H], "wb_plane")
-        scale_tab_d = zeroed_plane(nc.vector, [P, T], "scale_tab_d")
-        scale_tab_a = zeroed_plane(nc.vector, [P, T], "scale_tab_a")
-        wo_plane = zeroed_plane(nc.vector, [P, 2, N], "wo_plane")
+        table_scales_d = zeroed_plane(nc.vector, [P, T], "table_scales_d")
+        table_scales_a = zeroed_plane(nc.vector, [P, T], "table_scales_a")
+        wo_plane = zeroed_plane(nc.vector, [P, PASSES, N], "wo_plane")
+
+        table_words_b = load_table_words(tab2_words, "table_words_b")
         list_b = load_list(offs2, "list_b")
-        list_a = load_list(offs, "list_a")
         list_d = load_list(offs3, "list_d")
+        list_a = load_list(offs, "list_a")
         pick_b = load_list(pos2, "pick_b")
-        word_tab_b = load_table_words(tab2_words, "word_tab_b")
+        table_words_d = load_table_words(tab3_words, "table_words_d")
         wb_codes = keep.tile([P, 2 * H], U8, align_bytes=64)
         nc.sync.dma_start(out=wb_codes[:].bitcast(I32), in_=wb_words[0].bitcast(I32))
-        load_weight(wd, "d", 0, BANK // 2)
         pick_d = load_list(pos3, "pick_d")
-        load_scale_rows(nc.sync, scale_tab_b, tab2_scales[0], FIRST_SCALE_ROW["b"])
-        word_tab_d = load_table_words(tab3_words, "word_tab_d")
-        load_scale_rows(nc.sync, wb_plane, wb_scales[0])
-        load_weight(wd, "d", BANK // 2, BANK)
-        word_tab_a = load_table_words(tab_words, "word_tab_a")
-        load_scale_rows(nc.sync, scale_tab_d, tab3_scales[0], FIRST_SCALE_ROW["d"])
-        load_weight(wa, "a", 0, BANK)
-        load_scale_rows(nc.sync, scale_tab_a, tab_scales[0], FIRST_SCALE_ROW["a"])
-        load_weight(wd, "d", BANK, H)
-        load_weight(wa, "a", BANK, H)
+        load_scale_rows(table_scales_b, tab2_scales[0], FIRST_SCALE_ROW["b"])
+        table_words_a = load_table_words(tab_words, "table_words_a")
+        load_scale_rows(wb_plane, wb_scales[0])
+        load_weight(wd, "d", 0)
+        load_scale_rows(table_scales_d, tab3_scales[0], FIRST_SCALE_ROW["d"])
+        load_weight(wa, "a", 0)
+        load_scale_rows(table_scales_a, tab_scales[0], FIRST_SCALE_ROW["a"])
+        load_weight(wd, "d", 1)
+        load_weight(wa, "a", 1)
         pick_a = load_list(pos1, "pick_a")
-        wo_codes = keep.tile([P, 2, N], U32, align_bytes=64)
+        wo_codes = keep.tile([P, PASSES, N], U32, align_bytes=64)
         nc.sync.dma_start(out=wo_codes[:].bitcast(I32), in_=wo_words.rearrange("g p c i -> p g (c i)").bitcast(I32))
-        load_scale_rows(nc.sync, wo_plane, wo_scales.rearrange("g q c -> q g c"))
-        bias = keep.tile([P, N // P], F32)
+        load_scale_rows(wo_plane, wo_scales.rearrange("g q c -> q g c"))
+        bias = keep.tile([P, OUT_TILES], F32)
         with nc.allow_non_contiguous_dma(reason="one bias value for each partition"):
             nc.sync.dma_start(out=bias[:], in_=bo.rearrange("(c p) -> p c", p=P))
         identity = keep.tile([P, P], F32)
@@ -103,31 +117,30 @@ def tile_list_trio_pair_max_kernel(
 
         moving_words, moving_scales = {}, {}
 
-        def gather_table(name, words, plane, entries, pieces):
-            step = S // pieces
-            for lo in range(0, S, step):
-                part = entries[:, lo // 16 : (lo + step) // 16]
-                picked_words = keep.tile([P, step], U32, name=f"words_{name}{lo}", align_bytes=64)
-                nc.vector.tensor_copy(picked_words[:], words[:].indirect(part))
-                picked_scales = keep.tile([P, step], U8, name=f"scales_{name}{lo}", align_bytes=64)
-                nc.vector.tensor_copy(picked_scales[:], plane[:].indirect(part))
-                for at in range(0, step, BANK):
-                    moving_words[name, (lo + at) // BANK] = picked_words[:, at : at + BANK].bitcast(FP8X4)
-                    moving_scales[name, (lo + at) // BANK] = picked_scales[FIRST_SCALE_ROW[name] :, at : at + BANK]
+        def gather_table(name, words, plane, entries, scale_pieces):
+            found_words = keep.tile([P, S], U32, name=f"words_{name}", align_bytes=64)
+            nc.vector.tensor_copy(found_words[:], words[:].indirect(entries[:]))
+            width = S // scale_pieces
+            for lo in range(0, S, width):
+                found_scales = keep.tile([P, width], U8, name=f"scales_{name}{lo}", align_bytes=64)
+                nc.vector.tensor_copy(found_scales[:], plane[:].indirect(entries[:, lo // GROUP : (lo + width) // GROUP]))
+                for at in range(0, width, BANK):
+                    half = (lo + at) // BANK
+                    moving_words[name, half] = found_words[:, lo + at : lo + at + BANK].bitcast(FP8X4)
+                    moving_scales[name, half] = found_scales[FIRST_SCALE_ROW[name] :, at : at + BANK]
 
-        gather_table("b", word_tab_b, scale_tab_b, list_b, 2)
-        gather_table("d", word_tab_d, scale_tab_d, list_d, 1)
-        gather_table("a", word_tab_a, scale_tab_a, list_a, 1)
+        gather_table("b", table_words_b, table_scales_b, list_b, scale_pieces=2)
+        gather_table("d", table_words_d, table_scales_d, list_d, scale_pieces=1)
+        gather_table("a", table_words_a, table_scales_a, list_a, scale_pieces=1)
 
         rounded, codes, planes = {}, {}, {}
 
-        def round_weight(name, lo, hi):
-            g, at = divmod(lo, BANK)
-            if at == 0:
-                rounded[name, g] = keep.tile([P, BANK, PACK], BF16, name=f"rounded_{name}{g}", align_bytes=64)
+        def round_weight(name, g, lo=0, hi=PASS):
+            if lo == 0:
+                rounded[name, g] = keep.tile([P, PASS, PACK], BF16, name=f"rounded_{name}{g}", align_bytes=64)
             nc.scalar.activation(
-                out=rounded[name, g][:, at : at + hi - lo, :].rearrange("p (c e) i -> p c i e", e=4),
-                in_=raw[name, lo, hi][:].rearrange("p i (c e) -> p c i e", e=4),
+                out=rounded[name, g][:, lo:hi, :].rearrange("p (c e) i -> p c i e", e=4),
+                in_=raw[name, g][:, :, lo:hi].rearrange("p i (c e) -> p c i e", e=4),
                 func=ACT.Copy,
             )
 
@@ -135,11 +148,17 @@ def tile_list_trio_pair_max_kernel(
             width = values.shape[1]
             words = keep.tile([P, width], U32, name=f"codes_{name}", align_bytes=64)
             plane = keep.tile([P, width], U8, name=f"plane_{name}", align_bytes=64)
-            nc.vector.quantize_mx(out=words[:].bitcast(FP8X4), scales=plane[:], in_=values[:].rearrange("p c i -> p (c i)"))
+            nc.vector.quantize_mx(
+                out=words[:].bitcast(FP8X4), scales=plane[:], in_=values[:].rearrange("p c i -> p (c i)")
+            )
             return words, plane
 
-        def quantise_weight(name, half):
-            codes[name, half], planes[name, half] = quantise(rounded[name, half], f"{name}{half}")
+        def quantise_weight(name, g):
+            codes[name, g], planes[name, g] = quantise(rounded[name, g], f"{name}{g}")
+
+        def place_in_pass(t):
+            g, at = divmod(t, TILES_A_PASS)
+            return g, slice(P * at, P * (at + 1))
 
         features = {}
 
@@ -148,14 +167,14 @@ def tile_list_trio_pair_max_kernel(
                 lhs = wb_codes[:, 2 * P * t : 2 * P * (t + 1)].bitcast(FP4X4)
                 lhs_plane = wb_plane[:, P * t : P * (t + 1)]
             else:
-                g, cols = t // TILES_A_PASS, slice(P * (t % TILES_A_PASS), P * (t % TILES_A_PASS + 1))
+                g, cols = place_in_pass(t)
                 lhs = codes[name, g][:, cols].bitcast(FP8X4)
                 lhs_plane = planes[name, g][:, cols]
-            if half == 0 and name == "b" and t >= 6:
-                features[name, t] = reused.tile([P, S], F32, name=f"rows_b{t}", offset=(t - 6) * S * 4)
+            if half == 0 and name == "b" and t >= OWN_B_TILES:
+                features[name, t] = reused.tile([P, S], F32, name=f"rows_b{t}", offset=(t - OWN_B_TILES) * S * 4)
             elif half == 0:
-                features[name, t] = ring.tile([P, S], F32, name=f"rows_{name}", bufs=6 if name == "b" else 3)
-            acc = psum.tile([P, BANK], F32, name="acc", bufs=4)
+                features[name, t] = ring.tile([P, S], F32, name=f"rows_{name}", bufs=OWN_B_TILES if name == "b" else 3)
+            acc = psum.tile([P, BANK], F32, name="acc", bufs=ACC_BANKS)
             nc.tensor.matmul_mx(
                 out=acc[:], lhsT=lhs, lhsT_scale=lhs_plane,
                 rhs=moving_words[name, half], rhs_scale=moving_scales[name, half], start=True, stop=True,
@@ -163,143 +182,156 @@ def tile_list_trio_pair_max_kernel(
             nc.scalar.copy(out=features[name, t][:, half * BANK : (half + 1) * BANK], in_=acc[:])
 
         def first_stage(name, t):
-            for half in range(2):
+            for half in range(S // BANK):
                 first_stage_half(name, t, half)
 
         picked = {}
-        picks = {"a": pick_a, "b": pick_b, "d": pick_d}
+        pick_lists = {"a": pick_a, "b": pick_b, "d": pick_d}
 
-        def pick(name, t, blocks=slice(0, BLOCKS)):
+        def pick(name, t, blocks=ALL_BLOCKS):
             if blocks.start == 0:
                 picked[name, t] = ring.tile([P, J], F32, name=f"picked_{name}", bufs=ROW_TILES if name == "b" else 3)
             lo, hi = blocks.start * P, blocks.stop * P
-            nc.vector.tensor_copy(picked[name, t][:, lo:hi], features[name, t][:].indirect(picks[name][:, lo // 16 : hi // 16]))
+            entries = pick_lists[name][:, lo // GROUP : hi // GROUP]
+            nc.vector.tensor_copy(picked[name, t][:, lo:hi], features[name, t][:].indirect(entries))
 
-        def larger_of_b_d(t, blocks=slice(0, BLOCKS)):
-            if blocks.start == 0:
-                picked["m", t] = ring.tile([P, J], F32, name="larger")
-            cols = slice(blocks.start * P, blocks.stop * P)
-            nc.vector.tensor_tensor(picked["m", t][:, cols], picked["b", t][:, cols], picked["d", t][:, cols], MAX)
+        def pick_d_and_compare(t):
+            for blocks in BLOCK_PAIRS:
+                pick("d", t, blocks)
+            larger = ring.tile([P, J], F32)
+            for blocks in BLOCK_PAIRS:
+                cols = slice(blocks.start * P, blocks.stop * P)
+                nc.vector.tensor_tensor(larger[:, cols], picked["b", t][:, cols], picked["d", t][:, cols], MAX)
+            picked["larger", t] = larger
 
         def turned_sum(first, second, t, blocks, tag):
             total = psum.tile([P, blocks.stop - blocks.start, P], F32, name=tag)
             for at, block in enumerate(range(blocks.start, blocks.stop)):
                 cols = slice(block * P, (block + 1) * P)
-                nc.tensor.matmul(total[:, at, :], picked[first, t][:, cols], identity[:], is_transpose=True, start=True, stop=False)
-                nc.tensor.matmul(total[:, at, :], picked[second, t][:, cols], identity[:], is_transpose=True, start=False, stop=True)
+                for term in (first, second):
+                    nc.tensor.matmul(
+                        total[:, at, :], picked[term, t][:, cols], identity[:],
+                        is_transpose=True, start=(term == first), stop=(term == second),
+                    )
             return total
 
-        sums = {}
+        sums_b_d, sums_with_a = {}, {}
 
         def sum_b_d(t):
-            total = turned_sum("b", "d", t, slice(0, BLOCKS), "spare")
-            sums["s", t] = ring.tile([P, BLOCKS, P], F32, name="sum_bd")
-            nc.scalar.copy(out=sums["s", t][:], in_=total[:])
+            total = turned_sum("b", "d", t, ALL_BLOCKS, "spare")
+            sums_b_d[t] = ring.tile([P, BLOCKS, P], F32, name="sum_bd")
+            nc.scalar.copy(out=sums_b_d[t][:], in_=total[:])
 
-        def sum_with_a(t, blocks):
-            sums["t", t, blocks.start] = turned_sum("m", "a", t, blocks, "with_a")
+        def sum_with_a(t, blocks=ALL_BLOCKS):
+            sums_with_a[t, blocks.start] = turned_sum("larger", "a", t, blocks, "with_a")
 
-        z_turned = [keep.tile([P, BLOCKS * BANK], BF16, name=f"z_turned{g}") for g in range(2)]
+        z_turned = [keep.tile([P, BLOCKS * PASS], BF16, name=f"z_turned{g}") for g in range(PASSES)]
 
-        def finish_z(t, blocks=slice(0, BLOCKS)):
-            g, cols = t // TILES_A_PASS, slice(P * (t % TILES_A_PASS), P * (t % TILES_A_PASS + 1))
+        def finish_z(t, blocks=ALL_BLOCKS):
+            g, cols = place_in_pass(t)
             target = z_turned[g][:].rearrange("p (b r) -> p b r", b=BLOCKS)[:, blocks, cols]
-            nc.vector.tensor_tensor(target, sums["t", t, blocks.start][:], sums["s", t][:, blocks, :], MAX)
+            nc.vector.tensor_tensor(target, sums_with_a[t, blocks.start][:], sums_b_d[t][:, blocks, :], MAX)
 
-        def turn_back(g, blocks, target, copy):
+        def turn_back(g, blocks, target, copy, back):
             pairs = z_turned[g][:].bitcast(F32)
             count = blocks.stop - blocks.start
-            back = psum.tile([P, count, 2, P], F32, name="spare")
             for at in range(count):
-                lo = (blocks.start + at) * BANK // 2
+                lo = (blocks.start + at) * PASS // 2
                 for u in range(2):
-                    nc.tensor.transpose(back[:, at, u, :], pairs[:, lo + u : lo + BANK // 2 : 2], identity[:])
+                    nc.tensor.transpose(back[:, at, u, :], pairs[:, lo + u : lo + PASS // 2 : 2], identity[:])
             copy(
                 out=target.bitcast(F32).rearrange("p (b j) u -> p b j u", b=count),
                 in_=back[:].rearrange("p b u j -> p b j u"),
             )
 
-        def open_banks(width):
-            per_bank = min(BANK // width, N // P)
-            slots = []
-            for lo in range(0, N // P, per_bank):
-                bank = psum.tile([P, BANK], F32, name="acc", bufs=4)
-                count = min(per_bank, N // P - lo)
-                slots.extend((bank[:, at * width : (at + 1) * width], at == 0, at == count - 1) for at in range(count))
-            return slots
-
-        def second_stage_pass(slots, g, z_words, z_plane):
-            for c, (acc, first, final) in enumerate(slots):
+        def second_stage_pass(bank, g, z_words, z_plane):
+            for c in range(OUT_TILES):
                 cols = slice(c * P, (c + 1) * P)
                 nc.tensor.matmul_mx(
-                    out=acc, lhsT=wo_codes[:, g, cols].bitcast(FP8X4), lhsT_scale=wo_plane[:, g, cols],
+                    out=bank[:, c, :], lhsT=wo_codes[:, g, cols].bitcast(FP8X4), lhsT_scale=wo_plane[:, g, cols],
                     rhs=z_words.bitcast(FP8X4), rhs_scale=z_plane,
-                    start=(g == 0 and first), stop=(g == 1 and final),
+                    start=(g == 0 and c == 0), stop=(g == PASSES - 1 and c == OUT_TILES - 1),
                 )
 
-        def finish(slots, blocks):
-            cols = slice(blocks.start * P, blocks.stop * P)
-            result = keep.tile([P, N // P, cols.stop - cols.start], F32, name=f"result{blocks.start}")
-            for c, (acc, first, final) in enumerate(slots):
-                nc.scalar.activation(out=result[:, c, :], in_=acc, func=ACT.Tanh, bias=bias[:, c : c + 1])
-            nc.sync.dma_start(out=out[:, cols].rearrange("(c p) j -> p c j", p=P), in_=result[:])
+        def finish(bank, block):
+            cols = slice(block * P, (block + 1) * P)
+            result = keep.tile([P, OUT_TILES, P], F32, name=f"result{block}")
+            for c in range(OUT_TILES):
+                nc.scalar.activation(out=result[:, c, :], in_=bank[:, c, :], func=ACT.Tanh, bias=bias[:, c : c + 1])
+                if block == BLOCKS - 1:
+                    nc.sync.dma_start(out=out[c * P : (c + 1) * P, cols], in_=result[:, c, :])
+            if block < BLOCKS - 1:
+                nc.sync.dma_start(out=out[:, cols].rearrange("(c p) j -> p c j", p=P), in_=result[:])
 
-        round_weight("d", 0, BANK // 2)
-        for t in range(4):
+        for t in range(ACC_BANKS):
             first_stage_half("b", t, 0)
         for t in range(ROW_TILES):
-            if t >= 4:
+            if t >= ACC_BANKS:
                 first_stage_half("b", t, 0)
             first_stage_half("b", t, 1)
-            if t == 1:
-                round_weight("d", BANK // 2, BANK)
-            if t == 5:
-                round_weight("a", 0, BANK)
+            if t == ROUND_D_AFTER:
+                round_weight("d", 0)
+            if t == OWN_B_TILES - 1:
+                round_weight("a", 0)
                 quantise_weight("d", 0)
                 quantise_weight("a", 0)
             pick("b", t)
-        for name in "da":
-            round_weight(name, BANK, H)
-            quantise_weight(name, 1)
+        round_weight("d", 1)
+        quantise_weight("d", 1)
+
         first_stage("d", 0)
         first_stage("a", 0)
         last = ROW_TILES - 1
         z_rounded = keep.tile([P, J, PACK], BF16, align_bytes=64)
         for t in range(last):
-            pick("d", t)
-            larger_of_b_d(t)
+            pick_d_and_compare(t)
             pick("a", t)
             if t > 0:
                 finish_z(t - 1)
             first_stage("d", t + 1)
             first_stage("a", t + 1)
             sum_b_d(t)
-            sum_with_a(t, slice(0, BLOCKS))
+            sum_with_a(t)
+            if t < LATE_PIECES:
+                round_weight("a", 1, t * PASS // LATE_PIECES, (t + 1) * PASS // LATE_PIECES)
+            if t == LATE_PIECES:
+                quantise_weight("a", 1)
             if t == TILES_A_PASS:
-                for lo in range(0, BLOCKS, 2):
-                    turn_back(0, slice(lo, lo + 2), z_rounded[:, lo * P : (lo + 2) * P, :], nc.scalar.copy)
+                for blocks in BLOCK_PAIRS:
+                    back = psum.tile([P, 2, 2, P], F32, name="spare")
+                    turn_back(0, blocks, z_rounded[:, blocks.start * P : blocks.stop * P, :], nc.scalar.copy, back)
             if t == TILES_A_PASS + 1:
                 z_words, z_plane = quantise(z_rounded, "z")
-        pick("d", last)
-        larger_of_b_d(last)
+
+        early, late = (range(blocks.start, blocks.stop) for blocks in BLOCK_PAIRS)
+        pick_d_and_compare(last)
         sum_b_d(last)
-        slots = {}
-        for blocks in TAIL:
-            cols = slice(blocks.start * P, blocks.stop * P)
-            slots[blocks.start] = open_banks(cols.stop - cols.start)
-            second_stage_pass(slots[blocks.start], 0, z_words[:, cols], z_plane[:, cols])
-        for blocks in TAIL:
-            pick("a", last, blocks)
-            if blocks.start == 0:
+        banks = {}
+
+        def open_second_stage(block, bank):
+            cols = slice(block * P, (block + 1) * P)
+            banks[block] = bank
+            second_stage_pass(bank, 0, z_words[:, cols], z_plane[:, cols])
+
+        for block in late:
+            open_second_stage(block, psum.tile([P, OUT_TILES, P], F32, name="acc", bufs=ACC_BANKS))
+        for block in range(BLOCKS):
+            pick("a", last, slice(block, block + 1))
+            if block == 0:
                 finish_z(last - 1)
-            sum_with_a(last, blocks)
-        tail_rounded = {}
-        for blocks in TAIL:
-            finish_z(last, blocks)
-            width = (blocks.stop - blocks.start) * P
-            tail_rounded[blocks.start] = keep.tile([P, width, PACK], BF16, name=f"tail_rounded{blocks.start}", align_bytes=64)
-            turn_back(1, blocks, tail_rounded[blocks.start][:], nc.scalar.copy if blocks.start == 0 else nc.vector.tensor_copy)
-        for blocks in TAIL:
-            tail_words, tail_plane = quantise(tail_rounded[blocks.start], f"tail{blocks.start}")
-            second_stage_pass(slots[blocks.start], 1, tail_words[:], tail_plane[:])
-            finish(slots[blocks.start], blocks)
+            sum_with_a(last, slice(block, block + 1))
+        last_rounded = {}
+        for block in range(BLOCKS):
+            finish_z(last, slice(block, block + 1))
+            last_rounded[block] = keep.tile([P, P, PACK], BF16, name=f"last_rounded{block}", align_bytes=64)
+            if block in early:
+                back, copy = psum.tile([P, 1, 2, P], F32, name="spare"), nc.scalar.copy
+            else:
+                back, copy = psum.tile([P, 1, 2, P], F32, name="acc", bufs=ACC_BANKS), nc.vector.tensor_copy
+            turn_back(1, slice(block, block + 1), last_rounded[block][:], copy, back)
+        for block in early:
+            open_second_stage(block, psum.tile([P, OUT_TILES, P], F32, name="with_a"))
+        for block in range(BLOCKS):
+            last_words, last_plane = quantise(last_rounded[block], f"last{block}")
+            second_stage_pass(banks[block], 1, last_words[:], last_plane[:])
+            finish(banks[block], block)

from contextlib import ExitStack

import concourse.mybir as mybir
from concourse.masks import make_identity

K, T, S, J, H, N = 512, 2048, 1024, 512, 1024, 384
FLOPS = 2 * (3 * K * H * S + H * N * J)

F32 = mybir.dt.float32
BF16 = mybir.dt.bfloat16
I32 = mybir.dt.int32
U32 = mybir.dt.uint32
U16 = mybir.dt.uint16
U8 = mybir.dt.uint8
FP8X4 = mybir.dt.float8_e4m3fn_x4
FP4X4 = mybir.dt.float4_e2m1fn_x4
ACT = mybir.ActivationFunctionType
MAX = mybir.AluOpType.max

P = 128
PACK = 4
PASS = P * PACK
BANK = 512
GROUP = 16
PASSES = H // PASS
ROW_TILES = H // P
TILES_A_PASS = PASS // P
BLOCKS = J // P
ALL_BLOCKS = slice(0, BLOCKS)
BLOCK_PAIRS = (slice(0, 2), slice(2, 4))
OUT_TILES = N // P

FIRST_SCALE_ROW = {"a": 4, "b": 0, "d": 8}

ACC_BANKS = 4
OWN_B_TILES = 6
ROUND_D_AFTER = 1
LATE_PIECES = 2


def tile_list_trio_pair_max_kernel(
    tc, tab_words, tab_scales, tab2_words, tab2_scales, tab3_words, tab3_scales,
    offs, offs2, offs3, pos1, pos2, pos3, wa, wb_words, wb_scales, wd, wo_words, wo_scales, bo, out,
):
    nc = tc.nc
    with ExitStack() as ctx:
        keep = ctx.enter_context(tc.tile_pool(name="keep", bufs=1))
        ring = ctx.enter_context(tc.tile_pool(name="ring", bufs=3))
        reused = ctx.enter_context(tc.tile_pool(name="reused", bufs=1))
        psum = ctx.enter_context(tc.psum_pool(name="psum", bufs=2))

        raw = {}

        def load_list(dram, name):
            tile = keep.tile(list(dram.shape), U16, name=name)
            nc.sync.dma_start(tile[:], dram)
            return tile

        def zeroed_plane(engine, shape, name):
            plane = keep.tile(shape, U8, name=name, align_bytes=64)
            engine.memset(plane[:].bitcast(I32), 0)
            return plane

        def load_scale_rows(plane, rows, first=0):
            for quadrant in range(4):
                lo = 32 * quadrant + first
                nc.sync.dma_start(
                    out=plane[lo : lo + 4].bitcast(I32), in_=rows[4 * quadrant : 4 * quadrant + 4].bitcast(I32)
                )

        def load_table_words(dram, name):
            words = keep.tile([P, T], U32, name=name, align_bytes=64)
            nc.sync.dma_start(out=words[:].bitcast(I32), in_=dram[0].rearrange("p t i -> p (t i)").bitcast(I32))
            return words

        def load_weight(dram, name, g):
            if (name, g) == ("a", 0):
                raw[name, g] = reused.tile([P, PACK, PASS], F32, name="raw_a0", offset=0)
            else:
                raw[name, g] = keep.tile([P, PACK, PASS], F32, name=f"raw_{name}{g}")
            columns = dram[:, g * PASS : (g + 1) * PASS]
            nc.sync.dma_start(out=raw[name, g][:], in_=columns.rearrange("(p i) c -> p i c", i=PACK))

        table_scales_b = zeroed_plane(nc.gpsimd, [P, T], "table_scales_b")
        wb_plane = zeroed_plane(nc.gpsimd, [P, H], "wb_plane")
        table_scales_d = zeroed_plane(nc.vector, [P, T], "table_scales_d")
        table_scales_a = zeroed_plane(nc.vector, [P, T], "table_scales_a")
        wo_plane = zeroed_plane(nc.vector, [P, PASSES, N], "wo_plane")

        table_words_b = load_table_words(tab2_words, "table_words_b")
        list_b = load_list(offs2, "list_b")
        list_d = load_list(offs3, "list_d")
        list_a = load_list(offs, "list_a")
        pick_b = load_list(pos2, "pick_b")
        table_words_d = load_table_words(tab3_words, "table_words_d")
        wb_codes = keep.tile([P, 2 * H], U8, align_bytes=64)
        nc.sync.dma_start(out=wb_codes[:].bitcast(I32), in_=wb_words[0].bitcast(I32))
        pick_d = load_list(pos3, "pick_d")
        load_scale_rows(table_scales_b, tab2_scales[0], FIRST_SCALE_ROW["b"])
        table_words_a = load_table_words(tab_words, "table_words_a")
        load_scale_rows(wb_plane, wb_scales[0])
        load_weight(wd, "d", 0)
        load_scale_rows(table_scales_d, tab3_scales[0], FIRST_SCALE_ROW["d"])
        load_weight(wa, "a", 0)
        load_scale_rows(table_scales_a, tab_scales[0], FIRST_SCALE_ROW["a"])
        load_weight(wd, "d", 1)
        load_weight(wa, "a", 1)
        pick_a = load_list(pos1, "pick_a")
        wo_codes = keep.tile([P, PASSES, N], U32, align_bytes=64)
        nc.sync.dma_start(out=wo_codes[:].bitcast(I32), in_=wo_words.rearrange("g p c i -> p g (c i)").bitcast(I32))
        load_scale_rows(wo_plane, wo_scales.rearrange("g q c -> q g c"))
        bias = keep.tile([P, OUT_TILES], F32)
        with nc.allow_non_contiguous_dma(reason="one bias value for each partition"):
            nc.sync.dma_start(out=bias[:], in_=bo.rearrange("(c p) -> p c", p=P))
        identity = keep.tile([P, P], F32)
        make_identity(nc, identity[:])

        moving_words, moving_scales = {}, {}

        def gather_table(name, words, plane, entries, scale_pieces):
            found_words = keep.tile([P, S], U32, name=f"words_{name}", align_bytes=64)
            nc.vector.tensor_copy(found_words[:], words[:].indirect(entries[:]))
            width = S // scale_pieces
            for lo in range(0, S, width):
                found_scales = keep.tile([P, width], U8, name=f"scales_{name}{lo}", align_bytes=64)
                nc.vector.tensor_copy(found_scales[:], plane[:].indirect(entries[:, lo // GROUP : (lo + width) // GROUP]))
                for at in range(0, width, BANK):
                    half = (lo + at) // BANK
                    moving_words[name, half] = found_words[:, lo + at : lo + at + BANK].bitcast(FP8X4)
                    moving_scales[name, half] = found_scales[FIRST_SCALE_ROW[name] :, at : at + BANK]

        gather_table("b", table_words_b, table_scales_b, list_b, scale_pieces=2)
        gather_table("d", table_words_d, table_scales_d, list_d, scale_pieces=1)
        gather_table("a", table_words_a, table_scales_a, list_a, scale_pieces=1)

        rounded, codes, planes = {}, {}, {}

        def round_weight(name, g, lo=0, hi=PASS):
            if lo == 0:
                rounded[name, g] = keep.tile([P, PASS, PACK], BF16, name=f"rounded_{name}{g}", align_bytes=64)
            nc.scalar.activation(
                out=rounded[name, g][:, lo:hi, :].rearrange("p (c e) i -> p c i e", e=4),
                in_=raw[name, g][:, :, lo:hi].rearrange("p i (c e) -> p c i e", e=4),
                func=ACT.Copy,
            )

        def quantise(values, name):
            width = values.shape[1]
            words = keep.tile([P, width], U32, name=f"codes_{name}", align_bytes=64)
            plane = keep.tile([P, width], U8, name=f"plane_{name}", align_bytes=64)
            nc.vector.quantize_mx(
                out=words[:].bitcast(FP8X4), scales=plane[:], in_=values[:].rearrange("p c i -> p (c i)")
            )
            return words, plane

        def quantise_weight(name, g):
            codes[name, g], planes[name, g] = quantise(rounded[name, g], f"{name}{g}")

        def place_in_pass(t):
            g, at = divmod(t, TILES_A_PASS)
            return g, slice(P * at, P * (at + 1))

        features = {}

        def first_stage_half(name, t, half):
            if name == "b":
                lhs = wb_codes[:, 2 * P * t : 2 * P * (t + 1)].bitcast(FP4X4)
                lhs_plane = wb_plane[:, P * t : P * (t + 1)]
            else:
                g, cols = place_in_pass(t)
                lhs = codes[name, g][:, cols].bitcast(FP8X4)
                lhs_plane = planes[name, g][:, cols]
            if half == 0 and name == "b" and t >= OWN_B_TILES:
                features[name, t] = reused.tile([P, S], F32, name=f"rows_b{t}", offset=(t - OWN_B_TILES) * S * 4)
            elif half == 0:
                features[name, t] = ring.tile([P, S], F32, name=f"rows_{name}", bufs=OWN_B_TILES if name == "b" else 3)
            acc = psum.tile([P, BANK], F32, name="acc", bufs=ACC_BANKS)
            nc.tensor.matmul_mx(
                out=acc[:], lhsT=lhs, lhsT_scale=lhs_plane,
                rhs=moving_words[name, half], rhs_scale=moving_scales[name, half], start=True, stop=True,
            )
            nc.scalar.copy(out=features[name, t][:, half * BANK : (half + 1) * BANK], in_=acc[:])

        def first_stage(name, t):
            for half in range(S // BANK):
                first_stage_half(name, t, half)

        picked = {}
        pick_lists = {"a": pick_a, "b": pick_b, "d": pick_d}

        def pick(name, t, blocks=ALL_BLOCKS):
            if blocks.start == 0:
                picked[name, t] = ring.tile([P, J], F32, name=f"picked_{name}", bufs=ROW_TILES if name == "b" else 3)
            lo, hi = blocks.start * P, blocks.stop * P
            entries = pick_lists[name][:, lo // GROUP : hi // GROUP]
            nc.vector.tensor_copy(picked[name, t][:, lo:hi], features[name, t][:].indirect(entries))

        def pick_d_and_compare(t):
            for blocks in BLOCK_PAIRS:
                pick("d", t, blocks)
            larger = ring.tile([P, J], F32)
            for blocks in BLOCK_PAIRS:
                cols = slice(blocks.start * P, blocks.stop * P)
                nc.vector.tensor_tensor(larger[:, cols], picked["b", t][:, cols], picked["d", t][:, cols], MAX)
            picked["larger", t] = larger

        def turned_sum(first, second, t, blocks, tag):
            total = psum.tile([P, blocks.stop - blocks.start, P], F32, name=tag)
            for at, block in enumerate(range(blocks.start, blocks.stop)):
                cols = slice(block * P, (block + 1) * P)
                for term in (first, second):
                    nc.tensor.matmul(
                        total[:, at, :], picked[term, t][:, cols], identity[:],
                        is_transpose=True, start=(term == first), stop=(term == second),
                    )
            return total

        sums_b_d, sums_with_a = {}, {}

        def sum_b_d(t):
            total = turned_sum("b", "d", t, ALL_BLOCKS, "spare")
            sums_b_d[t] = ring.tile([P, BLOCKS, P], F32, name="sum_bd")
            nc.scalar.copy(out=sums_b_d[t][:], in_=total[:])

        def sum_with_a(t, blocks=ALL_BLOCKS):
            sums_with_a[t, blocks.start] = turned_sum("larger", "a", t, blocks, "with_a")

        z_turned = [keep.tile([P, BLOCKS * PASS], BF16, name=f"z_turned{g}") for g in range(PASSES)]

        def finish_z(t, blocks=ALL_BLOCKS):
            g, cols = place_in_pass(t)
            target = z_turned[g][:].rearrange("p (b r) -> p b r", b=BLOCKS)[:, blocks, cols]
            nc.vector.tensor_tensor(target, sums_with_a[t, blocks.start][:], sums_b_d[t][:, blocks, :], MAX)

        def turn_back(g, blocks, target, copy, back):
            pairs = z_turned[g][:].bitcast(F32)
            count = blocks.stop - blocks.start
            for at in range(count):
                lo = (blocks.start + at) * PASS // 2
                for u in range(2):
                    nc.tensor.transpose(back[:, at, u, :], pairs[:, lo + u : lo + PASS // 2 : 2], identity[:])
            copy(
                out=target.bitcast(F32).rearrange("p (b j) u -> p b j u", b=count),
                in_=back[:].rearrange("p b u j -> p b j u"),
            )

        def second_stage_pass(bank, g, z_words, z_plane):
            for c in range(OUT_TILES):
                cols = slice(c * P, (c + 1) * P)
                nc.tensor.matmul_mx(
                    out=bank[:, c, :], lhsT=wo_codes[:, g, cols].bitcast(FP8X4), lhsT_scale=wo_plane[:, g, cols],
                    rhs=z_words.bitcast(FP8X4), rhs_scale=z_plane,
                    start=(g == 0 and c == 0), stop=(g == PASSES - 1 and c == OUT_TILES - 1),
                )

        def finish(bank, block):
            cols = slice(block * P, (block + 1) * P)
            result = keep.tile([P, OUT_TILES, P], F32, name=f"result{block}")
            for c in range(OUT_TILES):
                nc.scalar.activation(out=result[:, c, :], in_=bank[:, c, :], func=ACT.Tanh, bias=bias[:, c : c + 1])
                if block == BLOCKS - 1:
                    nc.sync.dma_start(out=out[c * P : (c + 1) * P, cols], in_=result[:, c, :])
            if block < BLOCKS - 1:
                nc.sync.dma_start(out=out[:, cols].rearrange("(c p) j -> p c j", p=P), in_=result[:])

        for t in range(ACC_BANKS):
            first_stage_half("b", t, 0)
        for t in range(ROW_TILES):
            if t >= ACC_BANKS:
                first_stage_half("b", t, 0)
            first_stage_half("b", t, 1)
            if t == ROUND_D_AFTER:
                round_weight("d", 0)
            if t == OWN_B_TILES - 1:
                round_weight("a", 0)
                quantise_weight("d", 0)
                quantise_weight("a", 0)
            pick("b", t)
        round_weight("d", 1)
        quantise_weight("d", 1)

        first_stage("d", 0)
        first_stage("a", 0)
        last = ROW_TILES - 1
        z_rounded = keep.tile([P, J, PACK], BF16, align_bytes=64)
        for t in range(last):
            pick_d_and_compare(t)
            pick("a", t)
            if t > 0:
                finish_z(t - 1)
            first_stage("d", t + 1)
            first_stage("a", t + 1)
            sum_b_d(t)
            sum_with_a(t)
            if t < LATE_PIECES:
                round_weight("a", 1, t * PASS // LATE_PIECES, (t + 1) * PASS // LATE_PIECES)
            if t == LATE_PIECES:
                quantise_weight("a", 1)
            if t == TILES_A_PASS:
                for blocks in BLOCK_PAIRS:
                    back = psum.tile([P, 2, 2, P], F32, name="spare")
                    turn_back(0, blocks, z_rounded[:, blocks.start * P : blocks.stop * P, :], nc.scalar.copy, back)
            if t == TILES_A_PASS + 1:
                z_words, z_plane = quantise(z_rounded, "z")

        early, late = (range(blocks.start, blocks.stop) for blocks in BLOCK_PAIRS)
        pick_d_and_compare(last)
        sum_b_d(last)
        banks = {}

        def open_second_stage(block, bank):
            cols = slice(block * P, (block + 1) * P)
            banks[block] = bank
            second_stage_pass(bank, 0, z_words[:, cols], z_plane[:, cols])

        for block in late:
            open_second_stage(block, psum.tile([P, OUT_TILES, P], F32, name="acc", bufs=ACC_BANKS))
        for block in range(BLOCKS):
            pick("a", last, slice(block, block + 1))
            if block == 0:
                finish_z(last - 1)
            sum_with_a(last, slice(block, block + 1))
        last_rounded = {}
        for block in range(BLOCKS):
            finish_z(last, slice(block, block + 1))
            last_rounded[block] = keep.tile([P, P, PACK], BF16, name=f"last_rounded{block}", align_bytes=64)
            if block in early:
                back, copy = psum.tile([P, 1, 2, P], F32, name="spare"), nc.scalar.copy
            else:
                back, copy = psum.tile([P, 1, 2, P], F32, name="acc", bufs=ACC_BANKS), nc.vector.tensor_copy
            turn_back(1, slice(block, block + 1), last_rounded[block][:], copy, back)
        for block in early:
            open_second_stage(block, psum.tile([P, OUT_TILES, P], F32, name="with_a"))
        for block in range(BLOCKS):
            last_words, last_plane = quantise(last_rounded[block], f"last{block}")
            second_stage_pass(banks[block], 1, last_words[:], last_plane[:])
            finish(banks[block], block)
